import numpy as np
import ml_dtypes


def mxq(x, axis, fmt="e4m3"):
    dtype, down = {"e4m3": (ml_dtypes.float8_e4m3fn, 7), "e5m2": (ml_dtypes.float8_e5m2, 14)}[fmt]
    v = np.moveaxis(np.asarray(x, np.float32).astype(ml_dtypes.bfloat16).astype(np.float64), axis, -1)
    blocks = v.reshape(v.shape[:-1] + (-1, 32))
    amax = np.abs(blocks).max(-1, keepdims=True)
    byte = np.maximum(np.where(amax > 0, np.frexp(amax)[1] - 1 + 127, 0) - down, 1)
    scale = np.exp2(byte - 127.0)
    codes = (blocks / scale).astype(np.float32).astype(dtype).astype(np.float64)
    return np.moveaxis((codes * scale).reshape(v.shape), -1, axis)


WIDE = False


def mx_kscale(k):
    if not WIDE:
        return np.ones(k)
    levels = np.array([10, -10, 5, -5, 0])
    if k % 512:
        return np.exp2(np.random.permutation(np.resize(levels, k // 32))).repeat(32)
    a = np.empty((k // 512, 16))
    for p in range(k // 512):
        a[p, :8] = np.random.permutation(np.resize(levels, 8))
        for g in range(8):
            far = levels[np.abs(levels - a[p, g]) >= 10]
            a[p, g + 8] = far[np.random.randint(len(far))]
    return np.exp2(a.ravel()).repeat(32)


def f64(x):
    return np.asarray(x).astype(np.float64)


def striped(idx):
    return np.tile(np.asarray(idx).reshape(-1, 16).T, (8, 1)).astype(np.uint16)


def unstriped(offs):
    return offs[:16].T.reshape(-1).astype(np.int64)


E2M1 = np.array([0.0, 0.5, 1.0, 1.5, 2.0, 3.0, 4.0, 6.0, -0.0, -0.5, -1.0, -1.5, -2.0, -3.0, -4.0, -6.0])


def pack_weight(w, fmt):
    k, n = w.shape
    w = f64(np.asarray(w, np.float32).astype(ml_dtypes.bfloat16)).reshape(k // 32, 32, n)
    amax = np.abs(w).max(1)
    if fmt == "e4m3":
        byte = np.frexp(amax)[1] - 1 + 127 - 7
    else:
        mant, ex = np.frexp(amax / 6.0)
        byte = np.where(mant > 0.5, ex, ex - 1) + 127
    byte = np.clip(np.where(amax > 0, byte, 1), 1, 254)
    scaled = (w * np.exp2(127.0 - byte)[:, None, :]).reshape(k, n).astype(np.float32)
    by_word = np.ascontiguousarray(scaled.reshape(k // 512, 128, 4, n).transpose(0, 1, 3, 2))
    if fmt == "e4m3":
        words = by_word.astype(ml_dtypes.float8_e4m3fn).view(np.uint8)
    else:
        c = by_word.astype(ml_dtypes.float4_e2m1fn).view(np.uint8) & 0xF
        words = (c[..., 0::2] | (c[..., 1::2] << 4)).reshape(k // 512, 128, 2 * n)
    return np.ascontiguousarray(words), np.ascontiguousarray(byte.astype(np.uint8).reshape(k // 512, 16, n))


def unpack_weight(words, scales, fmt):
    g, _, n = scales.shape
    words = np.ascontiguousarray(words).reshape(g, 128, n, -1)
    if fmt == "e4m3":
        vals = words.view(ml_dtypes.float8_e4m3fn).astype(np.float64)
    else:
        nib = np.empty((g, 128, n, 4), np.uint8)
        nib[..., 0::2] = words & 0xF
        nib[..., 1::2] = words >> 4
        vals = E2M1[nib]
    vals = vals * np.repeat(np.exp2(scales.astype(np.float64) - 127.0), 8, axis=1)[..., None]
    return vals.transpose(0, 1, 3, 2).reshape(g * 512, n)


D, T, I, Q, E, U, G, K = 512, 2048, 512, 256, 512, 1024, 64, 32


def setup_inputs():
    n = np.random.standard_normal
    idx = np.random.permutation(T)[:I]
    idx2 = np.random.permutation(U)[:I]
    fd = mx_kscale(D)
    fi = mx_kscale(I)
    ti = np.ones(T)
    ti[idx] = fi
    keysp = pack_weight(n((D, T)) / fd[:, None], "e4m3")
    return {
        "query": (n((D, Q)) * 0.585 / np.sqrt(D) * fd[:, None]).astype(np.float32),
        "keys_words": keysp[0],
        "keys_scales": keysp[1],
        "concepts": (n((D, U)) / fd[:, None]).astype(np.float32),
        "part": np.tile(np.random.uniform(0.2, 1.0, T), (128, 1)).astype(np.float32),
        "lam": (np.random.uniform(0.7, 1.4, (Q, 1))).astype(np.float32),
        "shy": (np.random.uniform(20.0, 60.0, (Q, 1))).astype(np.float32),
        "os": (np.random.uniform(4.0, 16.0, (1, I)) * fi).astype(np.float32),
        "vals": (n((E, T)) / ti).astype(np.float32),
        "hold": (np.random.uniform(0.4, 1.0, (1, Q))).astype(np.float32),
        "offs": striped(idx),
        "offs2": striped(idx2),
    }


def reference(query, keys_words, keys_scales, concepts, part, lam, shy, os, vals, hold, offs, offs2):
    idx = unstriped(offs)
    idx2 = unstriped(offs2)
    keysu = unpack_weight(keys_words, keys_scales, "e4m3")
    queryq = mxq(f64(query), 0, "e4m3")
    keysidxg = keysu[:, idx]
    a = queryq.T @ keysidxg
    conceptsidx2q = mxq(f64(concepts)[:, idx2], 0, "e4m3")
    b = queryq.T @ conceptsidx2q
    s = (a - b * f64(part)[:1][:, idx]) * f64(lam)
    p = np.exp(s - np.max(s, axis=1, keepdims=True))
    r = p / np.sum(p, axis=1, keepdims=True)
    pg = r.reshape(Q, G, I // G).sum(axis=2)
    k0 = np.exp(pg * f64(shy) * (-1.0))
    kr = np.repeat(k0, I // G, axis=1)
    u0 = r * kr
    w = u0 / np.sum(u0, axis=1, keepdims=True)
    wo1 = w * f64(os)
    wt1 = wo1.T
    vt1 = f64(vals)[:, idx].T
    vt1q = mxq(vt1, 0, "e4m3")
    wt1q = mxq(wt1, 0, "e4m3")
    o = vt1q.T @ wt1q
    og = o.reshape(E, K, Q // K).mean(axis=2)
    ogr = np.repeat(og, Q // K, axis=1)
    y = o - ogr * f64(hold)
    return y

@@ -1,0 +1,297 @@
+from contextlib import ExitStack
+
+import concourse.mybir as mybir
+from concourse.masks import make_identity
+
+D, T, I, Q, E, U = 512, 2048, 512, 256, 512, 1024
+FLOPS = 2 * D * Q * I * 2 + 2 * I * E * Q
+
+F32 = mybir.dt.float32
+BF16 = mybir.dt.bfloat16
+I32 = mybir.dt.int32
+U32 = mybir.dt.uint32
+U16 = mybir.dt.uint16
+U8 = mybir.dt.uint8
+FP8X4 = mybir.dt.float8_e4m3fn_x4
+ALU = mybir.AluOpType
+ACT = mybir.ActivationFunctionType
+AXIS = mybir.AxisListType
+
+P = 128
+PACK = 4
+RUN = 8
+GROUP = 8
+HALF = I // 2
+LINE = 4
+
+
+def tile_attend_withoutconcept_crowdshy_beyondgroupread_kernel(
+    tc, query, keys_words, keys_scales, concepts, part, lam, shy, slot_factor, vals, hold, offs, offs2, out
+):
+    nc = tc.nc
+    q_tiles = Q // P
+    i_tiles = I // P
+    e_tiles = E // P
+
+    with ExitStack() as ctx:
+        sb = ctx.enter_context(tc.tile_pool(name="sb", bufs=1))
+        ps = ctx.enter_context(tc.psum_pool(name="ps", bufs=1))
+
+        def sbuf(name, shape, dtype, tag=None):
+            return sb.tile(shape, dtype, name=name, tag=tag or name, align_bytes=64)
+
+        def bank(number, name, shape):
+            return ps.tile(shape, F32, name=name, tag=f"bank{number}")
+
+        list_c = sb.tile([P, I // 16], U16, name="list_c")
+        list_t = sb.tile([P, I // 16], U16, name="list_t")
+        halves_c = [list_c[:, h * 16 : (h + 1) * 16] for h in range(2)]
+        halves_t = [list_t[:, h * 16 : (h + 1) * 16] for h in range(2)]
+
+        key_bytes = sbuf("key_bytes", [P, T], U8)
+        nc.gpsimd.memset(key_bytes[:].bitcast(I32), 0)
+        part_row = sbuf("part_row", [P, T], F32)
+        nc.vector.memset(part_row[:], 0.0)
+        ident = sbuf("ident", [P, P], F32)
+        make_identity(nc, ident[:])
+
+        q_raw = sbuf("q_raw", [P, PACK, Q], F32, "first")
+        planes = [sbuf(f"plane{t}", [P, U], F32, f"stage{t}") for t in range(PACK)]
+        concept_planes = concepts.rearrange("(p t) u -> t p u", t=PACK)
+        factor = sbuf("factor", [P, PACK], F32)
+        lam_cols = sbuf("lam_cols", [P, q_tiles], F32)
+        shy_cols = sbuf("shy_cols", [P, q_tiles], F32)
+        hold_cols = sbuf("hold_cols", [P, q_tiles], F32)
+
+        nc.sync.dma_start(list_c[:], offs2)
+        nc.sync.dma_start(list_t[:], offs)
+        nc.sync.dma_start(out=q_raw[:], in_=query.rearrange("(p t) q -> p t q", t=PACK))
+        for t in range(PACK):
+            nc.sync.dma_start(out=planes[t][:], in_=concept_planes[t])
+        nc.scalar.dma_start(out=factor[:], in_=slot_factor.rearrange("o (s r) -> (o s) r", r=PACK))
+        with nc.allow_non_contiguous_dma(reason="one value to a partition and tile of query rows"):
+            nc.scalar.dma_start(out=lam_cols[:], in_=lam.rearrange("(t p) o -> p (t o)", p=P))
+            nc.scalar.dma_start(out=shy_cols[:], in_=shy.rearrange("(t p) o -> p (t o)", p=P))
+            nc.scalar.dma_start(out=hold_cols[:], in_=hold.rearrange("o (t p) -> p (o t)", p=P))
+        for f in range(4):
+            nc.scalar.dma_start(
+                out=key_bytes[32 * f : 32 * f + 4, :].bitcast(I32), in_=keys_scales[0, 4 * f : 4 * f + 4, :].bitcast(I32)
+            )
+        nc.scalar.dma_start(out=part_row[0:1, :], in_=part[0:1, :])
+
+        def interleave(engine_copy, dst, src):
+            engine_copy(
+                dst.rearrange("p (c i) t -> p c t i", i=LINE), src.rearrange("p t (c i) -> p c t i", i=LINE)
+            )
+
+        def quantize(codes, scales, grouped):
+            nc.vector.quantize_mx(out=codes.bitcast(FP8X4), scales=scales, in_=grouped.rearrange("p c t -> p (c t)"))
+
+        def product(dst, lhs_codes, lhs_scales, rhs_codes, rhs_scales):
+            nc.tensor.matmul_mx(
+                out=dst, lhsT=lhs_codes.bitcast(FP8X4), lhsT_scale=lhs_scales,
+                rhs=rhs_codes.bitcast(FP8X4), rhs_scale=rhs_scales, start=True, stop=True,
+            )
+
+        def gather_vector(dst, window):
+            nc.vector.tensor_copy(dst, window)
+
+        def gather_scalar(dst, window):
+            nc.scalar.activation(dst, window, ACT.Copy)
+
+        q_grouped = sbuf("q_grouped", [P, Q, PACK], BF16)
+        q_codes = sbuf("q_codes", [P, Q], U32)
+        q_scales = sbuf("q_scales", [P, Q], U8)
+        interleave(nc.vector.tensor_copy, q_grouped[:], q_raw[:])
+        quantize(q_codes[:], q_scales[:], q_grouped[:])
+        key_words = sbuf("key_words", [P, T], I32, "first")
+        nc.sync.dma_start(out=key_words[:], in_=keys_words[0].rearrange("p n t -> p (n t)").bitcast(I32))
+
+        picked = sbuf("picked", [P, PACK, I], BF16)
+        picked_bytes = sbuf("picked_bytes", [P, I], U8)
+        picked_part = sbuf("picked_part", [P, I], F32)
+        v_raw = []
+
+        def load_values(e, tag):
+            v_raw.append(sbuf(f"v_raw{e}", [P, T], F32, tag))
+            nc.sync.dma_start(out=v_raw[e][:], in_=vals[e * P : (e + 1) * P, :])
+
+        gather_scalar(picked[:, 0, :], planes[0][:].indirect(list_c[:]))
+        load_values(0, "stage0")
+        gather_vector(picked[:, 1, :], planes[1][:].indirect(list_c[:]))
+        load_values(1, "stage1")
+        gather_scalar(picked_part[:], part_row[:].indirect(list_t[:]))
+        gather_vector(picked_bytes[:], key_bytes[:].indirect(list_t[:]))
+        gather_scalar(picked[:, 2, :], planes[2][:].indirect(list_c[:]))
+        load_values(2, "stage2")
+        gather_vector(picked[:, 3, 0:HALF], planes[3][:].indirect(halves_c[0]))
+        gather_scalar(picked[:, 3, HALF:I], planes[3][:].indirect(halves_c[1]))
+        load_values(3, "stage3")
+
+        neg_lam = sbuf("neg_lam", [P, q_tiles], F32)
+        nc.vector.tensor_scalar(neg_lam[:], lam_cols[:], -1.0, None, ALU.mult)
+        spread = bank(7, "spread", [P, Q])
+        for t in range(q_tiles):
+            nc.tensor.transpose(spread[:, t * P : (t + 1) * P], hold_cols[:, t : t + 1].to_broadcast([P, P]), ident[:])
+        neg_hold = sbuf("neg_hold", [P, Q], F32)
+        nc.vector.tensor_scalar(neg_hold[:], spread[:], -1.0 / GROUP, None, ALU.mult)
+        part_turned = bank(6, "part_turned", [P, i_tiles, P])
+        for j in range(i_tiles):
+            nc.tensor.transpose(part_turned[:, j, :], picked_part[:, j * P : (j + 1) * P], ident[:])
+        neg_part = sbuf("neg_part", [P, i_tiles], F32)
+        nc.scalar.activation(neg_part[:], part_turned[:, :, 0], ACT.Copy, scale=-1.0)
+
+        c_grouped = [sbuf(f"c_grouped{h}", [P, HALF, PACK], BF16) for h in range(2)]
+        c_codes = sbuf("c_codes", [P, I], U32)
+        c_scales = sbuf("c_scales", [P, I], U8)
+        interleave(nc.vector.tensor_copy, c_grouped[0][:], picked[:, :, 0:HALF])
+        interleave(nc.scalar.copy, c_grouped[1][:], picked[:, :, HALF:I])
+        b_banks = [bank(h, f"b_bank{h}", [P, 2, Q]) for h in range(2)]
+        neg_b = sbuf("neg_b", [P, i_tiles, Q], F32)
+        for h in range(2):
+            cols = slice(h * HALF, (h + 1) * HALF)
+            quantize(c_codes[:, cols], c_scales[:, cols], c_grouped[h][:])
+        for j in range(i_tiles):
+            cols = slice(j * P, (j + 1) * P)
+            product(b_banks[j // 2][:, j % 2, :], c_codes[:, cols], c_scales[:, cols], q_codes[:], q_scales[:])
+        for j in range(i_tiles):
+            nc.scalar.activation(neg_b[:, j, :], b_banks[j // 2][:, j % 2, :], ACT.Copy, scale=neg_part[:, j : j + 1])
+
+        picked_words = sbuf("picked_words", [P, I], U32)
+        a_banks = [bank(2 + h, f"a_bank{h}", [P, 2, Q]) for h in range(2)]
+        a_sb = [sbuf(f"a_sb{h}", [P, 2, Q], F32) for h in range(2)]
+        for h in range(2):
+            gather_vector(picked_words[:, h * HALF : (h + 1) * HALF], key_words[:].bitcast(U32).indirect(halves_t[h]))
+        for j in range(i_tiles):
+            cols = slice(j * P, (j + 1) * P)
+            product(a_banks[j // 2][:, j % 2, :], picked_words[:, cols], picked_bytes[:, cols], q_codes[:], q_scales[:])
+        nc.scalar.copy(a_sb[0][:], a_banks[0][:])
+        nc.vector.tensor_copy(a_sb[1][:], a_banks[1][:])
+
+        v_picked = []
+        v_grouped = [sbuf(f"v_grouped{e}", [P, P, PACK], BF16) for e in range(e_tiles)]
+        v_codes = [sbuf(f"v_codes{e}", [P, P], U32) for e in range(e_tiles)]
+        v_scales = [sbuf(f"v_scales{e}", [P, P], U8) for e in range(e_tiles)]
+
+        def gather_values(e, tag):
+            v_picked.append(sbuf(f"v_picked{e}", [P, I], BF16, tag))
+            if 0 < e < e_tiles - 1:
+                gather_scalar(v_picked[e][:], v_raw[e][:].indirect(list_t[:]))
+            else:
+                gather_vector(v_picked[e][:, 0:HALF], v_raw[e][:].indirect(halves_t[0]))
+                gather_scalar(v_picked[e][:, HALF:I], v_raw[e][:].indirect(halves_t[1]))
+
+        def turn_values(e):
+            pairs = v_picked[e][:].bitcast(F32)
+            v_bank = bank(7, f"v_bank{e}", [P, 2, P])
+            for u in range(2):
+                nc.tensor.transpose(v_bank[:, u, :], pairs[:, u : I // 2 : 2], ident[:])
+            nc.scalar.copy(
+                v_grouped[e][:].rearrange("s e r -> s (e r)").bitcast(F32).rearrange("s (e u) -> s e u", u=2),
+                v_bank[:].rearrange("s u e -> s e u"),
+            )
+
+        d_banks = [bank(4 + t, f"d_bank{t}", [P, I]) for t in range(q_tiles)]
+        for t in range(q_tiles):
+            for j in range(i_tiles):
+                nc.tensor.matmul(
+                    d_banks[t][:, j * P : (j + 1) * P], neg_b[:, j, t * P : (t + 1) * P], ident[:],
+                    start=(j == 0), stop=False, is_transpose=True,
+                )
+        for t in range(q_tiles):
+            for j in range(i_tiles):
+                nc.tensor.matmul(
+                    d_banks[t][:, j * P : (j + 1) * P], a_sb[j // 2][:, j % 2, t * P : (t + 1) * P], ident[:],
+                    start=False, stop=(j == i_tiles - 1), is_transpose=True,
+                )
+
+        gather_values(0, None)
+
+        def column(name):
+            return [sbuf(f"{name}{t}", [P, 1], F32) for t in range(q_tiles)]
+
+        neg_s = [sbuf(f"neg_s{t}", [P, PACK, P], F32, ("stage0", None)[t]) for t in range(q_tiles)]
+        p = [sbuf(f"p{t}", [P, I], F32) for t in range(q_tiles)]
+        neg_max, p_sum, p_inv, damp, u_sum, u_inv = [column(n) for n in ("neg_max", "p_sum", "p_inv", "damp", "u_sum", "u_inv")]
+        runs = [sbuf(f"runs{t}", [P, I // RUN], F32) for t in range(q_tiles)]
+        k0 = [sbuf(f"k0{t}", [P, I // RUN], F32) for t in range(q_tiles)]
+        damped = [sbuf(f"damped{t}", [P, I // RUN], F32) for t in range(q_tiles)]
+        kk = [sbuf(f"kk{t}", [P, I // RUN, 2], F32) for t in range(q_tiles)]
+
+        for t in range(q_tiles):
+            nc.vector.tensor_scalar(
+                neg_s[t][:], d_banks[t][:].rearrange("q (s r) -> q r s", r=PACK), neg_lam[:, t : t + 1], None,
+                ALU.mult, ALU.min, accum_out=neg_max[t][:],
+            )
+        for t in range(q_tiles):
+            nc.scalar.activation(
+                p[t][:], neg_s[t][:].rearrange("q r s -> q (r s)"), ACT.Exp, bias=neg_max[t][:], scale=-1.0,
+                accum_out=p_sum[t][:],
+            )
+        p_banks = [bank(h, f"p_bank{h}", [P, 2, Q]) for h in range(2)]
+        for t in range(q_tiles):
+            for r in range(PACK):
+                nc.tensor.transpose(p_banks[r // 2][:, r % 2, t * P : (t + 1) * P], p[t][:, r * P : (r + 1) * P], ident[:])
+        for t in range(q_tiles):
+            nc.vector.reciprocal(p_inv[t][:], p_sum[t][:])
+            nc.vector.tensor_reduce(
+                runs[t][:], p[t][:].rearrange("q (r g h) -> q g r h", r=PACK, h=2), AXIS.XY, ALU.add
+            )
+            nc.vector.tensor_scalar(damp[t][:], p_inv[t][:], shy_cols[:, t : t + 1], -1.0, ALU.mult, ALU.mult)
+            nc.scalar.activation(k0[t][:], runs[t][:], ACT.Exp, scale=damp[t][:])
+        scaled_p = sbuf("scaled_p", [P, PACK, Q], F32)
+        for r in range(PACK):
+            nc.scalar.activation(scaled_p[:, r, :], p_banks[r // 2][:, r % 2, :], ACT.Copy, scale=factor[:, r : r + 1])
+        for t in range(q_tiles):
+            nc.vector.scalar_tensor_tensor(damped[t][:], runs[t][:], 1.0, k0[t][:], ALU.mult, ALU.mult, accum_out=u_sum[t][:])
+        for t in range(q_tiles):
+            nc.vector.reciprocal(u_inv[t][:], u_sum[t][:])
+        k_bank = bank(6, "k_bank", [P, Q])
+        for t in range(q_tiles):
+            nc.vector.tensor_scalar(
+                kk[t][:], k0[t][:].unsqueeze(2).to_broadcast([P, I // RUN, 2]), u_inv[t][:], None, ALU.mult
+            )
+        for t in range(q_tiles):
+            nc.tensor.transpose(k_bank[:, t * P : (t + 1) * P], kk[t][:].rearrange("q g h -> q (g h)"), ident[:])
+
+        turn_values(0)
+        gather_values(1, "runs1")
+        turn_values(1)
+        gather_values(2, "k01")
+        turn_values(2)
+
+        w_grouped = [sbuf(f"w_grouped{t}", [P, P, PACK], BF16) for t in range(q_tiles)]
+        w_codes = sbuf("w_codes", [P, Q], U32)
+        w_scales = sbuf("w_scales", [P, Q], U8)
+        for t in range(q_tiles):
+            rows_q = slice(t * P, (t + 1) * P)
+            nc.vector.tensor_tensor(
+                w_grouped[t][:].rearrange("s (c i) r -> s c r i", i=LINE),
+                scaled_p[:, :, rows_q].rearrange("s r (c i) -> s c r i", i=LINE),
+                k_bank[:, rows_q].rearrange("s (c i) -> s c i", i=LINE).unsqueeze(2).to_broadcast([P, P // LINE, PACK, LINE]),
+                ALU.mult,
+            )
+        for t in range(q_tiles):
+            rows_q = slice(t * P, (t + 1) * P)
+            quantize(w_codes[:, rows_q], w_scales[:, rows_q], w_grouped[t][:])
+
+        def finish(e):
+            quantize(v_codes[e][:], v_scales[e][:], v_grouped[e][:])
+            o_bank = bank(2 + e, f"o_bank{e}", [P, Q])
+            product(o_bank[:], v_codes[e][:], v_scales[e][:], w_codes[:], w_scales[:])
+            sums = sbuf(f"sums{e}", [P, Q // GROUP], F32)
+            taken = sbuf(f"taken{e}", [P, Q // GROUP, GROUP], F32)
+            y = sbuf(f"y{e}", [P, Q], F32)
+            nc.vector.tensor_reduce(sums[:], o_bank[:].rearrange("e (k j) -> e k j", j=GROUP), AXIS.X, ALU.add)
+            engine = nc.gpsimd if e < e_tiles - 1 else nc.vector
+            engine.tensor_tensor(
+                taken[:], neg_hold[:].rearrange("e (k j) -> e k j", j=GROUP),
+                sums[:].unsqueeze(2).to_broadcast([P, Q // GROUP, GROUP]), ALU.mult,
+            )
+            nc.vector.tensor_tensor(y[:], o_bank[:], taken[:].rearrange("e k j -> e (k j)"), ALU.add)
+            nc.sync.dma_start(out=out[e * P : (e + 1) * P, :], in_=y[:])
+
+        gather_values(3, None)
+        turn_values(3)
+        for e in range(e_tiles):
+            finish(e)

@@ -48,36 +48,27 @@ def tile_attend_withoutconcept_crowdshy_beyondgroupread_kernel(
         halves_c = [list_c[:, h * 16 : (h + 1) * 16] for h in range(2)]
         halves_t = [list_t[:, h * 16 : (h + 1) * 16] for h in range(2)]
 
-        key_bytes = sbuf("key_bytes", [P, T], U8)
-        nc.gpsimd.memset(key_bytes[:].bitcast(I32), 0)
         part_row = sbuf("part_row", [P, T], F32)
         nc.vector.memset(part_row[:], 0.0)
+        key_bytes = sbuf("key_bytes", [P, T], U8)
+        nc.vector.memset(key_bytes[:].bitcast(I32), 0)
         ident = sbuf("ident", [P, P], F32)
         make_identity(nc, ident[:])
 
         q_raw = sbuf("q_raw", [P, PACK, Q], F32, "first")
         planes = [sbuf(f"plane{t}", [P, U], F32, f"stage{t}") for t in range(PACK)]
         concept_planes = concepts.rearrange("(p t) u -> t p u", t=PACK)
-        factor = sbuf("factor", [P, PACK], F32)
-        lam_cols = sbuf("lam_cols", [P, q_tiles], F32)
-        shy_cols = sbuf("shy_cols", [P, q_tiles], F32)
-        hold_cols = sbuf("hold_cols", [P, q_tiles], F32)
 
         nc.sync.dma_start(list_c[:], offs2)
         nc.sync.dma_start(list_t[:], offs)
         nc.sync.dma_start(out=q_raw[:], in_=query.rearrange("(p t) q -> p t q", t=PACK))
         for t in range(PACK):
             nc.sync.dma_start(out=planes[t][:], in_=concept_planes[t])
-        nc.scalar.dma_start(out=factor[:], in_=slot_factor.rearrange("o (s r) -> (o s) r", r=PACK))
-        with nc.allow_non_contiguous_dma(reason="one value to a partition and tile of query rows"):
-            nc.scalar.dma_start(out=lam_cols[:], in_=lam.rearrange("(t p) o -> p (t o)", p=P))
-            nc.scalar.dma_start(out=shy_cols[:], in_=shy.rearrange("(t p) o -> p (t o)", p=P))
-            nc.scalar.dma_start(out=hold_cols[:], in_=hold.rearrange("o (t p) -> p (o t)", p=P))
+        nc.scalar.dma_start(out=part_row[0:1, :], in_=part[0:1, :])
         for f in range(4):
             nc.scalar.dma_start(
                 out=key_bytes[32 * f : 32 * f + 4, :].bitcast(I32), in_=keys_scales[0, 4 * f : 4 * f + 4, :].bitcast(I32)
             )
-        nc.scalar.dma_start(out=part_row[0:1, :], in_=part[0:1, :])
 
         def interleave(engine_copy, dst, src):
             engine_copy(
@@ -99,13 +90,19 @@ def tile_attend_withoutconcept_crowdshy_beyondgroupread_kernel(
         def gather_scalar(dst, window):
             nc.scalar.activation(dst, window, ACT.Copy)
 
-        q_grouped = sbuf("q_grouped", [P, Q, PACK], BF16)
+        q_grouped = sbuf("q_grouped", [P, Q, PACK], BF16, "second")
         q_codes = sbuf("q_codes", [P, Q], U32)
         q_scales = sbuf("q_scales", [P, Q], U8)
         interleave(nc.vector.tensor_copy, q_grouped[:], q_raw[:])
         quantize(q_codes[:], q_scales[:], q_grouped[:])
         key_words = sbuf("key_words", [P, T], I32, "first")
         nc.sync.dma_start(out=key_words[:], in_=keys_words[0].rearrange("p n t -> p (n t)").bitcast(I32))
+        rows = sbuf("rows", [P, P], F32, "second")
+        nc.gpsimd.memset(rows[:], 0.0)
+        nc.sync.dma_start(out=rows[0:2, :], in_=lam.rearrange("(t p) o -> t (p o)", p=P))
+        nc.sync.dma_start(out=rows[2:4, :], in_=shy.rearrange("(t p) o -> t (p o)", p=P))
+        nc.sync.dma_start(out=rows[4:6, :], in_=hold.rearrange("o (t p) -> (o t) p", p=P))
+        nc.sync.dma_start(out=rows[6:10, :], in_=slot_factor.rearrange("o (j p) -> (o j) p", p=P))
 
         picked = sbuf("picked", [P, PACK, I], BF16)
         picked_bytes = sbuf("picked_bytes", [P, I], U8)
@@ -128,13 +125,6 @@ def tile_attend_withoutconcept_crowdshy_beyondgroupread_kernel(
         gather_scalar(picked[:, 3, HALF:I], planes[3][:].indirect(halves_c[1]))
         load_values(3, "stage3")
 
-        neg_lam = sbuf("neg_lam", [P, q_tiles], F32)
-        nc.vector.tensor_scalar(neg_lam[:], lam_cols[:], -1.0, None, ALU.mult)
-        spread = bank(7, "spread", [P, Q])
-        for t in range(q_tiles):
-            nc.tensor.transpose(spread[:, t * P : (t + 1) * P], hold_cols[:, t : t + 1].to_broadcast([P, P]), ident[:])
-        neg_hold = sbuf("neg_hold", [P, Q], F32)
-        nc.vector.tensor_scalar(neg_hold[:], spread[:], -1.0 / GROUP, None, ALU.mult)
         part_turned = bank(6, "part_turned", [P, i_tiles, P])
         for j in range(i_tiles):
             nc.tensor.transpose(part_turned[:, j, :], picked_part[:, j * P : (j + 1) * P], ident[:])
@@ -165,8 +155,15 @@ def tile_attend_withoutconcept_crowdshy_beyondgroupread_kernel(
         for j in range(i_tiles):
             cols = slice(j * P, (j + 1) * P)
             product(a_banks[j // 2][:, j % 2, :], picked_words[:, cols], picked_bytes[:, cols], q_codes[:], q_scales[:])
-        nc.scalar.copy(a_sb[0][:], a_banks[0][:])
-        nc.vector.tensor_copy(a_sb[1][:], a_banks[1][:])
+        for h in range(2):
+            nc.vector.tensor_copy(a_sb[h][:], a_banks[h][:])
+
+        turned = bank(7, "turned", [P, P])
+        nc.tensor.transpose(turned[:], rows[:], ident[:])
+        neg_cols = sbuf("neg_cols", [P, 4], F32)
+        cols_sb = sbuf("cols_sb", [P, 6], F32)
+        nc.scalar.activation(neg_cols[:], turned[:, 0:4], ACT.Copy, scale=-1.0)
+        nc.scalar.copy(cols_sb[:], turned[:, 4:10])
 
         v_picked = []
         v_grouped = [sbuf(f"v_grouped{e}", [P, P, PACK], BF16) for e in range(e_tiles)]
@@ -175,21 +172,21 @@ def tile_attend_withoutconcept_crowdshy_beyondgroupread_kernel(
 
         def gather_values(e, tag):
             v_picked.append(sbuf(f"v_picked{e}", [P, I], BF16, tag))
-            if 0 < e < e_tiles - 1:
-                gather_scalar(v_picked[e][:], v_raw[e][:].indirect(list_t[:]))
-            else:
-                gather_vector(v_picked[e][:, 0:HALF], v_raw[e][:].indirect(halves_t[0]))
-                gather_scalar(v_picked[e][:, HALF:I], v_raw[e][:].indirect(halves_t[1]))
+            gather_scalar(v_picked[e][:], v_raw[e][:].indirect(list_t[:]))
+
+        def turn_pairs(src, number, name, grouped):
+            pairs = src.bitcast(F32)
+            pair_bank = bank(number, name, [P, 2, P])
+            for u in range(2):
+                nc.tensor.transpose(pair_bank[:, u, :], pairs[:, u : I // 2 : 2], ident[:])
+            nc.scalar.copy(
+                grouped.rearrange("s x r -> s (x r)").bitcast(F32).rearrange("s (x u) -> s x u", u=2),
+                pair_bank[:].rearrange("s u x -> s x u"),
+            )
 
         def turn_values(e):
-            pairs = v_picked[e][:].bitcast(F32)
-            v_bank = bank(7, f"v_bank{e}", [P, 2, P])
-            for u in range(2):
-                nc.tensor.transpose(v_bank[:, u, :], pairs[:, u : I // 2 : 2], ident[:])
-            nc.scalar.copy(
-                v_grouped[e][:].rearrange("s e r -> s (e r)").bitcast(F32).rearrange("s (e u) -> s e u", u=2),
-                v_bank[:].rearrange("s u e -> s e u"),
-            )
+            turn_pairs(v_picked[e][:], 7 - e % 2, f"v_bank{e}", v_grouped[e][:])
+            quantize(v_codes[e][:], v_scales[e][:], v_grouped[e][:])
 
         d_banks = [bank(4 + t, f"d_bank{t}", [P, I]) for t in range(q_tiles)]
         for t in range(q_tiles):
@@ -205,93 +202,73 @@ def tile_attend_withoutconcept_crowdshy_beyondgroupread_kernel(
                     start=False, stop=(j == i_tiles - 1), is_transpose=True,
                 )
 
+        factor_bank = bank(2, "factor_bank", [P, I])
+        for j in range(i_tiles):
+            nc.tensor.transpose(factor_bank[:, j * P : (j + 1) * P], cols_sb[:, 2 + j : 3 + j].to_broadcast([P, P]), ident[:])
+        hold_bank = bank(3, "hold_bank", [P, Q])
+        for t in range(q_tiles):
+            nc.tensor.transpose(hold_bank[:, t * P : (t + 1) * P], cols_sb[:, t : t + 1].to_broadcast([P, P]), ident[:])
+
         gather_values(0, None)
 
         def column(name):
             return [sbuf(f"{name}{t}", [P, 1], F32) for t in range(q_tiles)]
 
-        neg_s = [sbuf(f"neg_s{t}", [P, PACK, P], F32, ("stage0", None)[t]) for t in range(q_tiles)]
-        p = [sbuf(f"p{t}", [P, I], F32) for t in range(q_tiles)]
+        neg_s = [sbuf(f"neg_s{t}", [P, I], F32) for t in range(q_tiles)]
+        p = [sbuf(f"p{t}", [P, I], F32, ("stage0", None)[t]) for t in range(q_tiles)]
         neg_max, p_sum, p_inv, damp, u_sum, u_inv = [column(n) for n in ("neg_max", "p_sum", "p_inv", "damp", "u_sum", "u_inv")]
         runs = [sbuf(f"runs{t}", [P, I // RUN], F32) for t in range(q_tiles)]
         k0 = [sbuf(f"k0{t}", [P, I // RUN], F32) for t in range(q_tiles)]
-        damped = [sbuf(f"damped{t}", [P, I // RUN], F32) for t in range(q_tiles)]
-        kk = [sbuf(f"kk{t}", [P, I // RUN, 2], F32) for t in range(q_tiles)]
+        damped = [sbuf(f"damped{t}", [P, I], F32) for t in range(q_tiles)]
+        w_rows = [sbuf(f"w_rows{t}", [P, I], BF16) for t in range(q_tiles)]
 
         for t in range(q_tiles):
             nc.vector.tensor_scalar(
-                neg_s[t][:], d_banks[t][:].rearrange("q (s r) -> q r s", r=PACK), neg_lam[:, t : t + 1], None,
-                ALU.mult, ALU.min, accum_out=neg_max[t][:],
+                neg_s[t][:], d_banks[t][:], neg_cols[:, t : t + 1], None, ALU.mult, ALU.min, accum_out=neg_max[t][:]
             )
         for t in range(q_tiles):
-            nc.scalar.activation(
-                p[t][:], neg_s[t][:].rearrange("q r s -> q (r s)"), ACT.Exp, bias=neg_max[t][:], scale=-1.0,
-                accum_out=p_sum[t][:],
-            )
-        p_banks = [bank(h, f"p_bank{h}", [P, 2, Q]) for h in range(2)]
-        for t in range(q_tiles):
-            for r in range(PACK):
-                nc.tensor.transpose(p_banks[r // 2][:, r % 2, t * P : (t + 1) * P], p[t][:, r * P : (r + 1) * P], ident[:])
+            nc.scalar.activation(p[t][:], neg_s[t][:], ACT.Exp, bias=neg_max[t][:], scale=-1.0, accum_out=p_sum[t][:])
+        turn_values(0)
         for t in range(q_tiles):
             nc.vector.reciprocal(p_inv[t][:], p_sum[t][:])
-            nc.vector.tensor_reduce(
-                runs[t][:], p[t][:].rearrange("q (r g h) -> q g r h", r=PACK, h=2), AXIS.XY, ALU.add
-            )
-            nc.vector.tensor_scalar(damp[t][:], p_inv[t][:], shy_cols[:, t : t + 1], -1.0, ALU.mult, ALU.mult)
+            nc.vector.tensor_reduce(runs[t][:], p[t][:].rearrange("q (g j) -> q g j", j=RUN), AXIS.X, ALU.add)
+            nc.vector.tensor_scalar(damp[t][:], p_inv[t][:], neg_cols[:, 2 + t : 3 + t], None, ALU.mult)
             nc.scalar.activation(k0[t][:], runs[t][:], ACT.Exp, scale=damp[t][:])
-        scaled_p = sbuf("scaled_p", [P, PACK, Q], F32)
-        for r in range(PACK):
-            nc.scalar.activation(scaled_p[:, r, :], p_banks[r // 2][:, r % 2, :], ACT.Copy, scale=factor[:, r : r + 1])
         for t in range(q_tiles):
-            nc.vector.scalar_tensor_tensor(damped[t][:], runs[t][:], 1.0, k0[t][:], ALU.mult, ALU.mult, accum_out=u_sum[t][:])
+            nc.vector.scalar_tensor_tensor(
+                damped[t][:].rearrange("q (g j) -> q g j", j=RUN), p[t][:].rearrange("q (g j) -> q g j", j=RUN), 1.0,
+                k0[t][:].unsqueeze(2).to_broadcast([P, I // RUN, RUN]), ALU.mult, ALU.mult, accum_out=u_sum[t][:],
+            )
         for t in range(q_tiles):
             nc.vector.reciprocal(u_inv[t][:], u_sum[t][:])
-        k_bank = bank(6, "k_bank", [P, Q])
         for t in range(q_tiles):
-            nc.vector.tensor_scalar(
-                kk[t][:], k0[t][:].unsqueeze(2).to_broadcast([P, I // RUN, 2]), u_inv[t][:], None, ALU.mult
-            )
-        for t in range(q_tiles):
-            nc.tensor.transpose(k_bank[:, t * P : (t + 1) * P], kk[t][:].rearrange("q g h -> q (g h)"), ident[:])
-
-        turn_values(0)
-        gather_values(1, "runs1")
-        turn_values(1)
-        gather_values(2, "k01")
-        turn_values(2)
+            nc.vector.scalar_tensor_tensor(w_rows[t][:], damped[t][:], u_inv[t][:], factor_bank[:], ALU.mult, ALU.mult)
 
         w_grouped = [sbuf(f"w_grouped{t}", [P, P, PACK], BF16) for t in range(q_tiles)]
         w_codes = sbuf("w_codes", [P, Q], U32)
         w_scales = sbuf("w_scales", [P, Q], U8)
         for t in range(q_tiles):
             rows_q = slice(t * P, (t + 1) * P)
-            nc.vector.tensor_tensor(
-                w_grouped[t][:].rearrange("s (c i) r -> s c r i", i=LINE),
-                scaled_p[:, :, rows_q].rearrange("s r (c i) -> s c r i", i=LINE),
-                k_bank[:, rows_q].rearrange("s (c i) -> s c i", i=LINE).unsqueeze(2).to_broadcast([P, P // LINE, PACK, LINE]),
-                ALU.mult,
-            )
-        for t in range(q_tiles):
-            rows_q = slice(t * P, (t + 1) * P)
+            turn_pairs(w_rows[t][:], t, f"w_bank{t}", w_grouped[t][:])
             quantize(w_codes[:, rows_q], w_scales[:, rows_q], w_grouped[t][:])
 
-        def finish(e):
-            quantize(v_codes[e][:], v_scales[e][:], v_grouped[e][:])
-            o_bank = bank(2 + e, f"o_bank{e}", [P, Q])
+        gather_values(1, "runs1")
+        turn_values(1)
+        gather_values(2, "k01")
+        turn_values(2)
+        gather_values(3, "w_grouped1")
+        turn_values(3)
+
+        for e in range(e_tiles):
+            o_bank = bank((4, 5, 0, 1)[e], f"o_bank{e}", [P, Q])
             product(o_bank[:], v_codes[e][:], v_scales[e][:], w_codes[:], w_scales[:])
             sums = sbuf(f"sums{e}", [P, Q // GROUP], F32)
             taken = sbuf(f"taken{e}", [P, Q // GROUP, GROUP], F32)
             y = sbuf(f"y{e}", [P, Q], F32)
             nc.vector.tensor_reduce(sums[:], o_bank[:].rearrange("e (k j) -> e k j", j=GROUP), AXIS.X, ALU.add)
-            engine = nc.gpsimd if e < e_tiles - 1 else nc.vector
-            engine.tensor_tensor(
-                taken[:], neg_hold[:].rearrange("e (k j) -> e k j", j=GROUP),
-                sums[:].unsqueeze(2).to_broadcast([P, Q // GROUP, GROUP]), ALU.mult,
+            nc.vector.scalar_tensor_tensor(
+                taken[:], sums[:].unsqueeze(2).to_broadcast([P, Q // GROUP, GROUP]), 1.0 / GROUP,
+                hold_bank[:].rearrange("e (k j) -> e k j", j=GROUP), ALU.mult, ALU.mult,
             )
-            nc.vector.tensor_tensor(y[:], o_bank[:], taken[:].rearrange("e k j -> e (k j)"), ALU.add)
+            nc.vector.tensor_tensor(y[:], o_bank[:], taken[:].rearrange("e k j -> e (k j)"), ALU.subtract)
             nc.sync.dma_start(out=out[e * P : (e + 1) * P, :], in_=y[:])
-
-        gather_values(3, None)
-        turn_values(3)
-        for e in range(e_tiles):
-            finish(e)

@@ -48,10 +48,10 @@ def tile_attend_withoutconcept_crowdshy_beyondgroupread_kernel(
         halves_c = [list_c[:, h * 16 : (h + 1) * 16] for h in range(2)]
         halves_t = [list_t[:, h * 16 : (h + 1) * 16] for h in range(2)]
 
+        key_bytes = sbuf("key_bytes", [P, T], U8)
+        nc.gpsimd.memset(key_bytes[:].bitcast(I32), 0)
         part_row = sbuf("part_row", [P, T], F32)
         nc.vector.memset(part_row[:], 0.0)
-        key_bytes = sbuf("key_bytes", [P, T], U8)
-        nc.vector.memset(key_bytes[:].bitcast(I32), 0)
         ident = sbuf("ident", [P, P], F32)
         make_identity(nc, ident[:])
 
@@ -64,11 +64,11 @@ def tile_attend_withoutconcept_crowdshy_beyondgroupread_kernel(
         nc.sync.dma_start(out=q_raw[:], in_=query.rearrange("(p t) q -> p t q", t=PACK))
         for t in range(PACK):
             nc.sync.dma_start(out=planes[t][:], in_=concept_planes[t])
-        nc.scalar.dma_start(out=part_row[0:1, :], in_=part[0:1, :])
         for f in range(4):
             nc.scalar.dma_start(
                 out=key_bytes[32 * f : 32 * f + 4, :].bitcast(I32), in_=keys_scales[0, 4 * f : 4 * f + 4, :].bitcast(I32)
             )
+        nc.scalar.dma_start(out=part_row[0:1, :], in_=part[0:1, :])
 
         def interleave(engine_copy, dst, src):
             engine_copy(
@@ -97,16 +97,15 @@ def tile_attend_withoutconcept_crowdshy_beyondgroupread_kernel(
         quantize(q_codes[:], q_scales[:], q_grouped[:])
         key_words = sbuf("key_words", [P, T], I32, "first")
         nc.sync.dma_start(out=key_words[:], in_=keys_words[0].rearrange("p n t -> p (n t)").bitcast(I32))
-        rows = sbuf("rows", [P, P], F32, "second")
-        nc.gpsimd.memset(rows[:], 0.0)
+        small = sbuf("small", [P, P + PACK], F32, "second")
+        rows, factor = small[:, 0:P], small[:, P : P + PACK]
+        nc.sync.dma_start(out=factor, in_=slot_factor.rearrange("o (s r) -> (o s) r", r=PACK))
+        nc.vector.memset(rows, 0.0)
         nc.sync.dma_start(out=rows[0:2, :], in_=lam.rearrange("(t p) o -> t (p o)", p=P))
         nc.sync.dma_start(out=rows[2:4, :], in_=shy.rearrange("(t p) o -> t (p o)", p=P))
         nc.sync.dma_start(out=rows[4:6, :], in_=hold.rearrange("o (t p) -> (o t) p", p=P))
-        nc.sync.dma_start(out=rows[6:10, :], in_=slot_factor.rearrange("o (j p) -> (o j) p", p=P))
 
         picked = sbuf("picked", [P, PACK, I], BF16)
-        picked_bytes = sbuf("picked_bytes", [P, I], U8)
-        picked_part = sbuf("picked_part", [P, I], F32)
         v_raw = []
 
         def load_values(e, tag):
@@ -115,58 +114,66 @@ def tile_attend_withoutconcept_crowdshy_beyondgroupread_kernel(
 
         gather_scalar(picked[:, 0, :], planes[0][:].indirect(list_c[:]))
         load_values(0, "stage0")
+        picked_bytes = sbuf("picked_bytes", [P, I], U8)
+        gather_vector(picked_bytes[:], key_bytes[:].indirect(list_t[:]))
         gather_vector(picked[:, 1, :], planes[1][:].indirect(list_c[:]))
         load_values(1, "stage1")
-        gather_scalar(picked_part[:], part_row[:].indirect(list_t[:]))
-        gather_vector(picked_bytes[:], key_bytes[:].indirect(list_t[:]))
         gather_scalar(picked[:, 2, :], planes[2][:].indirect(list_c[:]))
         load_values(2, "stage2")
         gather_vector(picked[:, 3, 0:HALF], planes[3][:].indirect(halves_c[0]))
         gather_scalar(picked[:, 3, HALF:I], planes[3][:].indirect(halves_c[1]))
-        load_values(3, "stage3")
+        part_hi = sbuf("part_hi", [P, HALF], F32, "stage3")
+        part_lo = sbuf("part_lo", [P, HALF], F32, "key_bytes")
+        gather_vector(part_lo[:], part_row[:].indirect(halves_t[0]))
+        gather_scalar(part_hi[:], part_row[:].indirect(halves_t[1]))
 
-        part_turned = bank(6, "part_turned", [P, i_tiles, P])
-        for j in range(i_tiles):
-            nc.tensor.transpose(part_turned[:, j, :], picked_part[:, j * P : (j + 1) * P], ident[:])
-        neg_part = sbuf("neg_part", [P, i_tiles], F32)
-        nc.scalar.activation(neg_part[:], part_turned[:, :, 0], ACT.Copy, scale=-1.0)
-
-        c_grouped = [sbuf(f"c_grouped{h}", [P, HALF, PACK], BF16) for h in range(2)]
-        c_codes = sbuf("c_codes", [P, I], U32)
-        c_scales = sbuf("c_scales", [P, I], U8)
+        c_grouped = [sbuf(f"c_grouped{h}", [P, HALF, PACK], BF16, ("part_row", None)[h]) for h in range(2)]
         interleave(nc.vector.tensor_copy, c_grouped[0][:], picked[:, :, 0:HALF])
         interleave(nc.scalar.copy, c_grouped[1][:], picked[:, :, HALF:I])
         b_banks = [bank(h, f"b_bank{h}", [P, 2, Q]) for h in range(2)]
-        neg_b = sbuf("neg_b", [P, i_tiles, Q], F32)
-        for h in range(2):
-            cols = slice(h * HALF, (h + 1) * HALF)
-            quantize(c_codes[:, cols], c_scales[:, cols], c_grouped[h][:])
-        for j in range(i_tiles):
-            cols = slice(j * P, (j + 1) * P)
-            product(b_banks[j // 2][:, j % 2, :], c_codes[:, cols], c_scales[:, cols], q_codes[:], q_scales[:])
-        for j in range(i_tiles):
-            nc.scalar.activation(neg_b[:, j, :], b_banks[j // 2][:, j % 2, :], ACT.Copy, scale=neg_part[:, j : j + 1])
-
-        picked_words = sbuf("picked_words", [P, I], U32)
         a_banks = [bank(2 + h, f"a_bank{h}", [P, 2, Q]) for h in range(2)]
-        a_sb = [sbuf(f"a_sb{h}", [P, 2, Q], F32) for h in range(2)]
-        for h in range(2):
+        scaled_b = [sbuf(f"scaled_b{h}", [P, 2, Q], F32) for h in range(2)]
+        neg_d = [sbuf(f"neg_d{h}", [P, 2, Q], F32) for h in range(2)]
+        c_codes = sbuf("c_codes", [P, I], U32)
+        c_scales = sbuf("c_scales", [P, I], U8)
+        picked_words = sbuf("picked_words", [P, I], U32)
+        part_cols = sbuf("part_cols", [P, i_tiles], F32)
+
+        def concept_products(h):
+            half = slice(h * HALF, (h + 1) * HALF)
+            quantize(c_codes[:, half], c_scales[:, half], c_grouped[h][:])
+            for j in range(2):
+                cols = slice((2 * h + j) * P, (2 * h + j + 1) * P)
+                product(b_banks[h][:, j, :], c_codes[:, cols], c_scales[:, cols], q_codes[:], q_scales[:])
+
+        def key_products(h):
             gather_vector(picked_words[:, h * HALF : (h + 1) * HALF], key_words[:].bitcast(U32).indirect(halves_t[h]))
-        for j in range(i_tiles):
-            cols = slice(j * P, (j + 1) * P)
-            product(a_banks[j // 2][:, j % 2, :], picked_words[:, cols], picked_bytes[:, cols], q_codes[:], q_scales[:])
+            for j in range(2):
+                cols = slice((2 * h + j) * P, (2 * h + j + 1) * P)
+                product(a_banks[h][:, j, :], picked_words[:, cols], picked_bytes[:, cols], q_codes[:], q_scales[:])
+
+        concept_products(0)
+        part_turned = bank(6, "part_turned", [P, i_tiles, P])
+        for j in (2, 3, 0, 1):
+            nc.tensor.transpose(part_turned[:, j, :], (part_lo, part_hi)[j // 2][:, j % 2 * P : (j % 2 + 1) * P], ident[:])
+        load_values(3, "stage3")
+        nc.scalar.copy(part_cols[:], part_turned[:, :, 0])
+        key_products(0)
+        concept_products(1)
+        key_products(1)
         for h in range(2):
-            nc.vector.tensor_copy(a_sb[h][:], a_banks[h][:])
+            for j in range(2):
+                nc.scalar.activation(
+                    scaled_b[h][:, j, :], b_banks[h][:, j, :], ACT.Copy, scale=part_cols[:, 2 * h + j : 2 * h + j + 1]
+                )
+            nc.vector.tensor_tensor(neg_d[h][:], scaled_b[h][:], a_banks[h][:], ALU.subtract)
 
         turned = bank(7, "turned", [P, P])
-        nc.tensor.transpose(turned[:], rows[:], ident[:])
-        neg_cols = sbuf("neg_cols", [P, 4], F32)
+        nc.tensor.transpose(turned[:], rows, ident[:])
         cols_sb = sbuf("cols_sb", [P, 6], F32)
-        nc.scalar.activation(neg_cols[:], turned[:, 0:4], ACT.Copy, scale=-1.0)
-        nc.scalar.copy(cols_sb[:], turned[:, 4:10])
+        nc.vector.tensor_copy(cols_sb[:], turned[:, 0:6])
 
         v_picked = []
-        v_grouped = [sbuf(f"v_grouped{e}", [P, P, PACK], BF16) for e in range(e_tiles)]
         v_codes = [sbuf(f"v_codes{e}", [P, P], U32) for e in range(e_tiles)]
         v_scales = [sbuf(f"v_scales{e}", [P, P], U8) for e in range(e_tiles)]
 
@@ -174,90 +181,105 @@ def tile_attend_withoutconcept_crowdshy_beyondgroupread_kernel(
             v_picked.append(sbuf(f"v_picked{e}", [P, I], BF16, tag))
             gather_scalar(v_picked[e][:], v_raw[e][:].indirect(list_t[:]))
 
-        def turn_pairs(src, number, name, grouped):
+        def turn_pairs(src, number, name, grouped, copy):
             pairs = src.bitcast(F32)
             pair_bank = bank(number, name, [P, 2, P])
             for u in range(2):
                 nc.tensor.transpose(pair_bank[:, u, :], pairs[:, u : I // 2 : 2], ident[:])
-            nc.scalar.copy(
+            copy(
                 grouped.rearrange("s x r -> s (x r)").bitcast(F32).rearrange("s (x u) -> s x u", u=2),
                 pair_bank[:].rearrange("s u x -> s x u"),
             )
 
-        def turn_values(e):
-            turn_pairs(v_picked[e][:], 7 - e % 2, f"v_bank{e}", v_grouped[e][:])
-            quantize(v_codes[e][:], v_scales[e][:], v_grouped[e][:])
+        def turn_values(e, tag, copy):
+            v_grouped = sbuf(f"v_grouped{e}", [P, P, PACK], BF16, tag)
+            turn_pairs(v_picked[e][:], 7 - e % 2, f"v_bank{e}", v_grouped[:], copy)
+            quantize(v_codes[e][:], v_scales[e][:], v_grouped[:])
 
         d_banks = [bank(4 + t, f"d_bank{t}", [P, I]) for t in range(q_tiles)]
-        for t in range(q_tiles):
-            for j in range(i_tiles):
-                nc.tensor.matmul(
-                    d_banks[t][:, j * P : (j + 1) * P], neg_b[:, j, t * P : (t + 1) * P], ident[:],
-                    start=(j == 0), stop=False, is_transpose=True,
-                )
-        for t in range(q_tiles):
-            for j in range(i_tiles):
-                nc.tensor.matmul(
-                    d_banks[t][:, j * P : (j + 1) * P], a_sb[j // 2][:, j % 2, t * P : (t + 1) * P], ident[:],
-                    start=False, stop=(j == i_tiles - 1), is_transpose=True,
-                )
+        for h in range(2):
+            for t in range(q_tiles):
+                for j in range(2):
+                    cols = slice((2 * h + j) * P, (2 * h + j + 1) * P)
+                    nc.tensor.transpose(d_banks[t][:, cols], neg_d[h][:, j, t * P : (t + 1) * P], ident[:])
 
-        factor_bank = bank(2, "factor_bank", [P, I])
-        for j in range(i_tiles):
-            nc.tensor.transpose(factor_bank[:, j * P : (j + 1) * P], cols_sb[:, 2 + j : 3 + j].to_broadcast([P, P]), ident[:])
         hold_bank = bank(3, "hold_bank", [P, Q])
         for t in range(q_tiles):
-            nc.tensor.transpose(hold_bank[:, t * P : (t + 1) * P], cols_sb[:, t : t + 1].to_broadcast([P, P]), ident[:])
+            nc.tensor.transpose(hold_bank[:, t * P : (t + 1) * P], cols_sb[:, 4 + t : 5 + t].to_broadcast([P, P]), ident[:])
 
         gather_values(0, None)
+        gather_values(1, None)
 
         def column(name):
             return [sbuf(f"{name}{t}", [P, 1], F32) for t in range(q_tiles)]
 
-        neg_s = [sbuf(f"neg_s{t}", [P, I], F32) for t in range(q_tiles)]
-        p = [sbuf(f"p{t}", [P, I], F32, ("stage0", None)[t]) for t in range(q_tiles)]
+        neg_s = [sbuf(f"neg_s{t}", [P, PACK, P], F32) for t in range(q_tiles)]
+        p = []
         neg_max, p_sum, p_inv, damp, u_sum, u_inv = [column(n) for n in ("neg_max", "p_sum", "p_inv", "damp", "u_sum", "u_inv")]
-        runs = [sbuf(f"runs{t}", [P, I // RUN], F32) for t in range(q_tiles)]
-        k0 = [sbuf(f"k0{t}", [P, I // RUN], F32) for t in range(q_tiles)]
-        damped = [sbuf(f"damped{t}", [P, I], F32) for t in range(q_tiles)]
-        w_rows = [sbuf(f"w_rows{t}", [P, I], BF16) for t in range(q_tiles)]
+        runs = []
+        damped = [sbuf(f"damped{t}", [P, I // RUN], F32) for t in range(q_tiles)]
+        kk = [sbuf(f"kk{t}", [P, I // RUN, 2], F32) for t in range(q_tiles)]
 
         for t in range(q_tiles):
             nc.vector.tensor_scalar(
-                neg_s[t][:], d_banks[t][:], neg_cols[:, t : t + 1], None, ALU.mult, ALU.min, accum_out=neg_max[t][:]
+                neg_s[t][:], d_banks[t][:].rearrange("q (s r) -> q r s", r=PACK), cols_sb[:, t : t + 1], None,
+                ALU.mult, ALU.min, accum_out=neg_max[t][:],
             )
         for t in range(q_tiles):
-            nc.scalar.activation(p[t][:], neg_s[t][:], ACT.Exp, bias=neg_max[t][:], scale=-1.0, accum_out=p_sum[t][:])
-        turn_values(0)
+            p.append(sbuf(f"p{t}", [P, I], F32, ("stage1", "neg_s0")[t]))
+            nc.scalar.activation(
+                p[t][:], neg_s[t][:].rearrange("q r s -> q (r s)"), ACT.Exp, bias=neg_max[t][:], scale=-1.0,
+                accum_out=p_sum[t][:],
+            )
+        k0 = [sbuf(f"k0{t}", [P, I // RUN], F32) for t in range(q_tiles)]
+        p_banks = [bank(h, f"p_bank{h}", [P, 2, Q]) for h in range(2)]
+        for t in range(q_tiles):
+            for r in range(PACK):
+                nc.tensor.transpose(p_banks[r // 2][:, r % 2, t * P : (t + 1) * P], p[t][:, r * P : (r + 1) * P], ident[:])
         for t in range(q_tiles):
             nc.vector.reciprocal(p_inv[t][:], p_sum[t][:])
-            nc.vector.tensor_reduce(runs[t][:], p[t][:].rearrange("q (g j) -> q g j", j=RUN), AXIS.X, ALU.add)
-            nc.vector.tensor_scalar(damp[t][:], p_inv[t][:], neg_cols[:, 2 + t : 3 + t], None, ALU.mult)
-            nc.scalar.activation(k0[t][:], runs[t][:], ACT.Exp, scale=damp[t][:])
-        for t in range(q_tiles):
-            nc.vector.scalar_tensor_tensor(
-                damped[t][:].rearrange("q (g j) -> q g j", j=RUN), p[t][:].rearrange("q (g j) -> q g j", j=RUN), 1.0,
-                k0[t][:].unsqueeze(2).to_broadcast([P, I // RUN, RUN]), ALU.mult, ALU.mult, accum_out=u_sum[t][:],
+            runs.append(sbuf(f"runs{t}", [P, I // RUN], F32, ("p_sum0", "p_inv0")[t]))
+            nc.vector.tensor_reduce(
+                runs[t][:], p[t][:].rearrange("q (r g h) -> q g r h", r=PACK, h=2), AXIS.XY, ALU.add
             )
+            nc.vector.tensor_scalar(damp[t][:], p_inv[t][:], cols_sb[:, 2 + t : 3 + t], -1.0, ALU.mult, ALU.mult)
+            nc.scalar.activation(k0[t][:], runs[t][:], ACT.Exp, scale=damp[t][:])
+        turn_values(0, "p_inv1", nc.vector.tensor_copy)
+        scaled_p = sbuf("scaled_p", [P, PACK, Q], F32, "damp1")
+        for r in range(PACK):
+            nc.scalar.activation(scaled_p[:, r, :], p_banks[r // 2][:, r % 2, :], ACT.Copy, scale=factor[:, r : r + 1])
+        for t in range(q_tiles):
+            nc.vector.scalar_tensor_tensor(damped[t][:], runs[t][:], 1.0, k0[t][:], ALU.mult, ALU.mult, accum_out=u_sum[t][:])
         for t in range(q_tiles):
             nc.vector.reciprocal(u_inv[t][:], u_sum[t][:])
+        k_bank = bank(2, "k_bank", [P, Q])
         for t in range(q_tiles):
-            nc.vector.scalar_tensor_tensor(w_rows[t][:], damped[t][:], u_inv[t][:], factor_bank[:], ALU.mult, ALU.mult)
+            nc.vector.tensor_scalar(
+                kk[t][:], k0[t][:].unsqueeze(2).to_broadcast([P, I // RUN, 2]), u_inv[t][:], None, ALU.mult
+            )
+        for t in range(q_tiles):
+            nc.tensor.transpose(k_bank[:, t * P : (t + 1) * P], kk[t][:].rearrange("q g h -> q (g h)"), ident[:])
+
+        turn_values(1, "k01", nc.vector.tensor_copy)
+        gather_values(2, "p_inv0")
+        gather_values(3, "kk1")
+        turn_values(2, None, nc.scalar.copy)
+        turn_values(3, None, nc.scalar.copy)
 
         w_grouped = [sbuf(f"w_grouped{t}", [P, P, PACK], BF16) for t in range(q_tiles)]
         w_codes = sbuf("w_codes", [P, Q], U32)
         w_scales = sbuf("w_scales", [P, Q], U8)
         for t in range(q_tiles):
             rows_q = slice(t * P, (t + 1) * P)
-            turn_pairs(w_rows[t][:], t, f"w_bank{t}", w_grouped[t][:])
+            nc.vector.tensor_tensor(
+                w_grouped[t][:].rearrange("s (c i) r -> s c r i", i=LINE),
+                scaled_p[:, :, rows_q].rearrange("s r (c i) -> s c r i", i=LINE),
+                k_bank[:, rows_q].rearrange("s (c i) -> s c i", i=LINE).unsqueeze(2).to_broadcast([P, P // LINE, PACK, LINE]),
+                ALU.mult,
+            )
+        for t in range(q_tiles):
+            rows_q = slice(t * P, (t + 1) * P)
             quantize(w_codes[:, rows_q], w_scales[:, rows_q], w_grouped[t][:])
-
-        gather_values(1, "runs1")
-        turn_values(1)
-        gather_values(2, "k01")
-        turn_values(2)
-        gather_values(3, "w_grouped1")
-        turn_values(3)
 
         for e in range(e_tiles):
             o_bank = bank((4, 5, 0, 1)[e], f"o_bank{e}", [P, Q])

@@ -22,7 +22,9 @@ PACK = 4
 RUN = 8
 GROUP = 8
 HALF = I // 2
+LIST_ROWS = 16
 LINE = 4
+QUADRANT = 32
 
 
 def tile_attend_withoutconcept_crowdshy_beyondgroupread_kernel(
@@ -37,16 +39,17 @@ def tile_attend_withoutconcept_crowdshy_beyondgroupread_kernel(
         sb = ctx.enter_context(tc.tile_pool(name="sb", bufs=1))
         ps = ctx.enter_context(tc.psum_pool(name="ps", bufs=1))
 
-        def sbuf(name, shape, dtype, tag=None):
-            return sb.tile(shape, dtype, name=name, tag=tag or name, align_bytes=64)
+        def sbuf(name, shape, dtype, reuse=None):
+            return sb.tile(shape, dtype, name=name, tag=reuse or name, align_bytes=64)
 
         def bank(number, name, shape):
             return ps.tile(shape, F32, name=name, tag=f"bank{number}")
 
-        list_c = sb.tile([P, I // 16], U16, name="list_c")
-        list_t = sb.tile([P, I // 16], U16, name="list_t")
-        halves_c = [list_c[:, h * 16 : (h + 1) * 16] for h in range(2)]
-        halves_t = [list_t[:, h * 16 : (h + 1) * 16] for h in range(2)]
+        list_c = sb.tile([P, I // LIST_ROWS], U16, name="list_c")
+        list_t = sb.tile([P, I // LIST_ROWS], U16, name="list_t")
+        half_cols = HALF // LIST_ROWS
+        halves_c = [list_c[:, h * half_cols : (h + 1) * half_cols] for h in range(2)]
+        halves_t = [list_t[:, h * half_cols : (h + 1) * half_cols] for h in range(2)]
 
         key_bytes = sbuf("key_bytes", [P, T], U8)
         nc.gpsimd.memset(key_bytes[:].bitcast(I32), 0)
@@ -64,9 +67,10 @@ def tile_attend_withoutconcept_crowdshy_beyondgroupread_kernel(
         nc.sync.dma_start(out=q_raw[:], in_=query.rearrange("(p t) q -> p t q", t=PACK))
         for t in range(PACK):
             nc.sync.dma_start(out=planes[t][:], in_=concept_planes[t])
-        for f in range(4):
+        for f in range(P // QUADRANT):
             nc.scalar.dma_start(
-                out=key_bytes[32 * f : 32 * f + 4, :].bitcast(I32), in_=keys_scales[0, 4 * f : 4 * f + 4, :].bitcast(I32)
+                out=key_bytes[QUADRANT * f : QUADRANT * f + 4, :].bitcast(I32),
+                in_=keys_scales[0, 4 * f : 4 * f + 4, :].bitcast(I32),
             )
         nc.scalar.dma_start(out=part_row[0:1, :], in_=part[0:1, :])
 
@@ -95,6 +99,7 @@ def tile_attend_withoutconcept_crowdshy_beyondgroupread_kernel(
         q_scales = sbuf("q_scales", [P, Q], U8)
         interleave(nc.vector.tensor_copy, q_grouped[:], q_raw[:])
         quantize(q_codes[:], q_scales[:], q_grouped[:])
+
         key_words = sbuf("key_words", [P, T], I32, "first")
         nc.sync.dma_start(out=key_words[:], in_=keys_words[0].rearrange("p n t -> p (n t)").bitcast(I32))
         small = sbuf("small", [P, P + PACK], F32, "second")
@@ -108,8 +113,8 @@ def tile_attend_withoutconcept_crowdshy_beyondgroupread_kernel(
         picked = sbuf("picked", [P, PACK, I], BF16)
         v_raw = []
 
-        def load_values(e, tag):
-            v_raw.append(sbuf(f"v_raw{e}", [P, T], F32, tag))
+        def load_values(e, reuse):
+            v_raw.append(sbuf(f"v_raw{e}", [P, T], F32, reuse))
             nc.sync.dma_start(out=v_raw[e][:], in_=vals[e * P : (e + 1) * P, :])
 
         gather_scalar(picked[:, 0, :], planes[0][:].indirect(list_c[:]))
@@ -154,8 +159,9 @@ def tile_attend_withoutconcept_crowdshy_beyondgroupread_kernel(
 
         concept_products(0)
         part_turned = bank(6, "part_turned", [P, i_tiles, P])
-        for j in (2, 3, 0, 1):
-            nc.tensor.transpose(part_turned[:, j, :], (part_lo, part_hi)[j // 2][:, j % 2 * P : (j % 2 + 1) * P], ident[:])
+        for source, first_block in ((part_hi, 2), (part_lo, 0)):
+            for j in range(2):
+                nc.tensor.transpose(part_turned[:, first_block + j, :], source[:, j * P : (j + 1) * P], ident[:])
         load_values(3, "stage3")
         nc.scalar.copy(part_cols[:], part_turned[:, :, 0])
         key_products(0)
@@ -170,31 +176,32 @@ def tile_attend_withoutconcept_crowdshy_beyondgroupread_kernel(
 
         turned = bank(7, "turned", [P, P])
         nc.tensor.transpose(turned[:], rows, ident[:])
-        cols_sb = sbuf("cols_sb", [P, 6], F32)
-        nc.vector.tensor_copy(cols_sb[:], turned[:, 0:6])
+        cols_sb = sbuf("cols_sb", [P, 3 * q_tiles], F32)
+        nc.vector.tensor_copy(cols_sb[:], turned[:, 0 : 3 * q_tiles])
 
         v_picked = []
-        v_codes = [sbuf(f"v_codes{e}", [P, P], U32) for e in range(e_tiles)]
+        v_grouped = []
+        v_codes = []
         v_scales = [sbuf(f"v_scales{e}", [P, P], U8) for e in range(e_tiles)]
 
-        def gather_values(e, tag):
-            v_picked.append(sbuf(f"v_picked{e}", [P, I], BF16, tag))
+        def gather_values(e, reuse):
+            v_picked.append(sbuf(f"v_picked{e}", [P, I], BF16, reuse))
             gather_scalar(v_picked[e][:], v_raw[e][:].indirect(list_t[:]))
 
-        def turn_pairs(src, number, name, grouped, copy):
-            pairs = src.bitcast(F32)
-            pair_bank = bank(number, name, [P, 2, P])
+        def turn_values(e, reuse):
+            v_grouped.append(sbuf(f"v_grouped{e}", [P, P, PACK], BF16, reuse))
+            pairs = v_picked[e][:].bitcast(F32)
+            pair_bank = bank(7 - e % 2, f"v_bank{e}", [P, 2, P])
             for u in range(2):
                 nc.tensor.transpose(pair_bank[:, u, :], pairs[:, u : I // 2 : 2], ident[:])
-            copy(
-                grouped.rearrange("s x r -> s (x r)").bitcast(F32).rearrange("s (x u) -> s x u", u=2),
+            nc.scalar.copy(
+                v_grouped[e][:].rearrange("s x r -> s (x r)").bitcast(F32).rearrange("s (x u) -> s x u", u=2),
                 pair_bank[:].rearrange("s u x -> s x u"),
             )
 
-        def turn_values(e, tag, copy):
-            v_grouped = sbuf(f"v_grouped{e}", [P, P, PACK], BF16, tag)
-            turn_pairs(v_picked[e][:], 7 - e % 2, f"v_bank{e}", v_grouped[:], copy)
-            quantize(v_codes[e][:], v_scales[e][:], v_grouped[:])
+        def quantize_values(e, reuse):
+            v_codes.append(sbuf(f"v_codes{e}", [P, P], U32, reuse))
+            quantize(v_codes[e][:], v_scales[e][:], v_grouped[e][:])
 
         d_banks = [bank(4 + t, f"d_bank{t}", [P, I]) for t in range(q_tiles)]
         for h in range(2):
@@ -215,7 +222,9 @@ def tile_attend_withoutconcept_crowdshy_beyondgroupread_kernel(
 
         neg_s = [sbuf(f"neg_s{t}", [P, PACK, P], F32) for t in range(q_tiles)]
         p = []
-        neg_max, p_sum, p_inv, damp, u_sum, u_inv = [column(n) for n in ("neg_max", "p_sum", "p_inv", "damp", "u_sum", "u_inv")]
+        neg_max, p_sum, p_inv, damp, u_sum, u_inv = [
+            column(n) for n in ("neg_max", "p_sum", "p_inv", "damp", "u_sum", "u_inv")
+        ]
         runs = []
         damped = [sbuf(f"damped{t}", [P, I // RUN], F32) for t in range(q_tiles)]
         kk = [sbuf(f"kk{t}", [P, I // RUN, 2], F32) for t in range(q_tiles)]
@@ -232,10 +241,12 @@ def tile_attend_withoutconcept_crowdshy_beyondgroupread_kernel(
                 accum_out=p_sum[t][:],
             )
         k0 = [sbuf(f"k0{t}", [P, I // RUN], F32) for t in range(q_tiles)]
-        p_banks = [bank(h, f"p_bank{h}", [P, 2, Q]) for h in range(2)]
+        turn_values(0, "neg_s1")
+        turn_values(1, "neg_max1")
+        p_banks = [bank(t, f"p_bank{t}", [P, PACK, P]) for t in range(q_tiles)]
         for t in range(q_tiles):
             for r in range(PACK):
-                nc.tensor.transpose(p_banks[r // 2][:, r % 2, t * P : (t + 1) * P], p[t][:, r * P : (r + 1) * P], ident[:])
+                nc.tensor.transpose(p_banks[t][:, r, :], p[t][:, r * P : (r + 1) * P], ident[:])
         for t in range(q_tiles):
             nc.vector.reciprocal(p_inv[t][:], p_sum[t][:])
             runs.append(sbuf(f"runs{t}", [P, I // RUN], F32, ("p_sum0", "p_inv0")[t]))
@@ -244,45 +255,47 @@ def tile_attend_withoutconcept_crowdshy_beyondgroupread_kernel(
             )
             nc.vector.tensor_scalar(damp[t][:], p_inv[t][:], cols_sb[:, 2 + t : 3 + t], -1.0, ALU.mult, ALU.mult)
             nc.scalar.activation(k0[t][:], runs[t][:], ACT.Exp, scale=damp[t][:])
-        turn_values(0, "p_inv1", nc.vector.tensor_copy)
-        scaled_p = sbuf("scaled_p", [P, PACK, Q], F32, "damp1")
-        for r in range(PACK):
-            nc.scalar.activation(scaled_p[:, r, :], p_banks[r // 2][:, r % 2, :], ACT.Copy, scale=factor[:, r : r + 1])
+        quantize_values(0, "p_inv1")
+        scaled_p = [sbuf(f"scaled_p{t}", [P, PACK, P], F32, f"damp{t}") for t in range(q_tiles)]
+        for t in range(q_tiles):
+            for r in range(PACK):
+                nc.scalar.activation(scaled_p[t][:, r, :], p_banks[t][:, r, :], ACT.Copy, scale=factor[:, r : r + 1])
         for t in range(q_tiles):
             nc.vector.scalar_tensor_tensor(damped[t][:], runs[t][:], 1.0, k0[t][:], ALU.mult, ALU.mult, accum_out=u_sum[t][:])
         for t in range(q_tiles):
             nc.vector.reciprocal(u_inv[t][:], u_sum[t][:])
-        k_bank = bank(2, "k_bank", [P, Q])
+        quantize_values(1, "u_sum0")
+        k_banks = [bank(4 + t, f"k_bank{t}", [P, P]) for t in range(q_tiles)]
         for t in range(q_tiles):
             nc.vector.tensor_scalar(
                 kk[t][:], k0[t][:].unsqueeze(2).to_broadcast([P, I // RUN, 2]), u_inv[t][:], None, ALU.mult
             )
         for t in range(q_tiles):
-            nc.tensor.transpose(k_bank[:, t * P : (t + 1) * P], kk[t][:].rearrange("q g h -> q (g h)"), ident[:])
+            nc.tensor.transpose(k_banks[t][:], kk[t][:].rearrange("q g h -> q (g h)"), ident[:])
 
-        turn_values(1, "k01", nc.vector.tensor_copy)
         gather_values(2, "p_inv0")
         gather_values(3, "kk1")
-        turn_values(2, None, nc.scalar.copy)
-        turn_values(3, None, nc.scalar.copy)
+        for e in (2, 3):
+            turn_values(e, None)
+            quantize_values(e, None)
 
         w_grouped = [sbuf(f"w_grouped{t}", [P, P, PACK], BF16) for t in range(q_tiles)]
         w_codes = sbuf("w_codes", [P, Q], U32)
         w_scales = sbuf("w_scales", [P, Q], U8)
         for t in range(q_tiles):
-            rows_q = slice(t * P, (t + 1) * P)
             nc.vector.tensor_tensor(
                 w_grouped[t][:].rearrange("s (c i) r -> s c r i", i=LINE),
-                scaled_p[:, :, rows_q].rearrange("s r (c i) -> s c r i", i=LINE),
-                k_bank[:, rows_q].rearrange("s (c i) -> s c i", i=LINE).unsqueeze(2).to_broadcast([P, P // LINE, PACK, LINE]),
+                scaled_p[t][:].rearrange("s r (c i) -> s c r i", i=LINE),
+                k_banks[t][:].rearrange("s (c i) -> s c i", i=LINE).unsqueeze(2).to_broadcast([P, P // LINE, PACK, LINE]),
                 ALU.mult,
             )
         for t in range(q_tiles):
             rows_q = slice(t * P, (t + 1) * P)
             quantize(w_codes[:, rows_q], w_scales[:, rows_q], w_grouped[t][:])
 
+        o_bank_numbers = (2, 4, 0, 1)
         for e in range(e_tiles):
-            o_bank = bank((4, 5, 0, 1)[e], f"o_bank{e}", [P, Q])
+            o_bank = bank(o_bank_numbers[e], f"o_bank{e}", [P, Q])
             product(o_bank[:], v_codes[e][:], v_scales[e][:], w_codes[:], w_scales[:])
             sums = sbuf(f"sums{e}", [P, Q // GROUP], F32)
             taken = sbuf(f"taken{e}", [P, Q // GROUP, GROUP], F32)

from contextlib import ExitStack

import concourse.mybir as mybir
from concourse.masks import make_identity

D, T, I, Q, E, U = 512, 2048, 512, 256, 512, 1024
FLOPS = 2 * D * Q * I * 2 + 2 * I * E * Q

F32 = mybir.dt.float32
BF16 = mybir.dt.bfloat16
I32 = mybir.dt.int32
U32 = mybir.dt.uint32
U16 = mybir.dt.uint16
U8 = mybir.dt.uint8
FP8X4 = mybir.dt.float8_e4m3fn_x4
ALU = mybir.AluOpType
ACT = mybir.ActivationFunctionType
AXIS = mybir.AxisListType

P = 128
PACK = 4
RUN = 8
GROUP = 8
HALF = I // 2
LIST_ROWS = 16
LINE = 4
QUADRANT = 32


def tile_attend_withoutconcept_crowdshy_beyondgroupread_kernel(
    tc, query, keys_words, keys_scales, concepts, part, lam, shy, slot_factor, vals, hold, offs, offs2, out
):
    nc = tc.nc
    q_tiles = Q // P
    i_tiles = I // P
    e_tiles = E // P

    with ExitStack() as ctx:
        sb = ctx.enter_context(tc.tile_pool(name="sb", bufs=1))
        ps = ctx.enter_context(tc.psum_pool(name="ps", bufs=1))

        def sbuf(name, shape, dtype, reuse=None):
            return sb.tile(shape, dtype, name=name, tag=reuse or name, align_bytes=64)

        def bank(number, name, shape):
            return ps.tile(shape, F32, name=name, tag=f"bank{number}")

        list_c = sb.tile([P, I // LIST_ROWS], U16, name="list_c")
        list_t = sb.tile([P, I // LIST_ROWS], U16, name="list_t")
        half_cols = HALF // LIST_ROWS
        halves_c = [list_c[:, h * half_cols : (h + 1) * half_cols] for h in range(2)]
        halves_t = [list_t[:, h * half_cols : (h + 1) * half_cols] for h in range(2)]

        key_bytes = sbuf("key_bytes", [P, T], U8)
        nc.gpsimd.memset(key_bytes[:].bitcast(I32), 0)
        part_row = sbuf("part_row", [P, T], F32)
        nc.vector.memset(part_row[:], 0.0)
        ident = sbuf("ident", [P, P], F32)
        make_identity(nc, ident[:])

        q_raw = sbuf("q_raw", [P, PACK, Q], F32, "first")
        planes = [sbuf(f"plane{t}", [P, U], F32, f"stage{t}") for t in range(PACK)]
        concept_planes = concepts.rearrange("(p t) u -> t p u", t=PACK)

        nc.sync.dma_start(list_c[:], offs2)
        nc.sync.dma_start(list_t[:], offs)
        nc.sync.dma_start(out=q_raw[:], in_=query.rearrange("(p t) q -> p t q", t=PACK))
        for t in range(PACK):
            nc.sync.dma_start(out=planes[t][:], in_=concept_planes[t])
        for f in range(P // QUADRANT):
            nc.scalar.dma_start(
                out=key_bytes[QUADRANT * f : QUADRANT * f + 4, :].bitcast(I32),
                in_=keys_scales[0, 4 * f : 4 * f + 4, :].bitcast(I32),
            )
        nc.scalar.dma_start(out=part_row[0:1, :], in_=part[0:1, :])

        def interleave(engine_copy, dst, src):
            engine_copy(
                dst.rearrange("p (c i) t -> p c t i", i=LINE), src.rearrange("p t (c i) -> p c t i", i=LINE)
            )

        def quantize(codes, scales, grouped):
            nc.vector.quantize_mx(out=codes.bitcast(FP8X4), scales=scales, in_=grouped.rearrange("p c t -> p (c t)"))

        def product(dst, lhs_codes, lhs_scales, rhs_codes, rhs_scales):
            nc.tensor.matmul_mx(
                out=dst, lhsT=lhs_codes.bitcast(FP8X4), lhsT_scale=lhs_scales,
                rhs=rhs_codes.bitcast(FP8X4), rhs_scale=rhs_scales, start=True, stop=True,
            )

        def gather_vector(dst, window):
            nc.vector.tensor_copy(dst, window)

        def gather_scalar(dst, window):
            nc.scalar.activation(dst, window, ACT.Copy)

        q_grouped = sbuf("q_grouped", [P, Q, PACK], BF16, "second")
        q_codes = sbuf("q_codes", [P, Q], U32)
        q_scales = sbuf("q_scales", [P, Q], U8)
        interleave(nc.vector.tensor_copy, q_grouped[:], q_raw[:])
        quantize(q_codes[:], q_scales[:], q_grouped[:])

        key_words = sbuf("key_words", [P, T], I32, "first")
        nc.sync.dma_start(out=key_words[:], in_=keys_words[0].rearrange("p n t -> p (n t)").bitcast(I32))
        small = sbuf("small", [P, P + PACK], F32, "second")
        rows, factor = small[:, 0:P], small[:, P : P + PACK]
        nc.sync.dma_start(out=factor, in_=slot_factor.rearrange("o (s r) -> (o s) r", r=PACK))
        nc.vector.memset(rows, 0.0)
        nc.sync.dma_start(out=rows[0:2, :], in_=lam.rearrange("(t p) o -> t (p o)", p=P))
        nc.sync.dma_start(out=rows[2:4, :], in_=shy.rearrange("(t p) o -> t (p o)", p=P))
        nc.sync.dma_start(out=rows[4:6, :], in_=hold.rearrange("o (t p) -> (o t) p", p=P))

        picked = sbuf("picked", [P, PACK, I], BF16)
        v_raw = []

        def load_values(e, reuse):
            v_raw.append(sbuf(f"v_raw{e}", [P, T], F32, reuse))
            nc.sync.dma_start(out=v_raw[e][:], in_=vals[e * P : (e + 1) * P, :])

        gather_scalar(picked[:, 0, :], planes[0][:].indirect(list_c[:]))
        load_values(0, "stage0")
        picked_bytes = sbuf("picked_bytes", [P, I], U8)
        gather_vector(picked_bytes[:], key_bytes[:].indirect(list_t[:]))
        gather_vector(picked[:, 1, :], planes[1][:].indirect(list_c[:]))
        load_values(1, "stage1")
        gather_scalar(picked[:, 2, :], planes[2][:].indirect(list_c[:]))
        load_values(2, "stage2")
        gather_vector(picked[:, 3, 0:HALF], planes[3][:].indirect(halves_c[0]))
        gather_scalar(picked[:, 3, HALF:I], planes[3][:].indirect(halves_c[1]))
        part_hi = sbuf("part_hi", [P, HALF], F32, "stage3")
        part_lo = sbuf("part_lo", [P, HALF], F32, "key_bytes")
        gather_vector(part_lo[:], part_row[:].indirect(halves_t[0]))
        gather_scalar(part_hi[:], part_row[:].indirect(halves_t[1]))

        c_grouped = [sbuf(f"c_grouped{h}", [P, HALF, PACK], BF16, ("part_row", None)[h]) for h in range(2)]
        interleave(nc.vector.tensor_copy, c_grouped[0][:], picked[:, :, 0:HALF])
        interleave(nc.scalar.copy, c_grouped[1][:], picked[:, :, HALF:I])
        b_banks = [bank(h, f"b_bank{h}", [P, 2, Q]) for h in range(2)]
        a_banks = [bank(2 + h, f"a_bank{h}", [P, 2, Q]) for h in range(2)]
        scaled_b = [sbuf(f"scaled_b{h}", [P, 2, Q], F32) for h in range(2)]
        neg_d = [sbuf(f"neg_d{h}", [P, 2, Q], F32) for h in range(2)]
        c_codes = sbuf("c_codes", [P, I], U32)
        c_scales = sbuf("c_scales", [P, I], U8)
        picked_words = sbuf("picked_words", [P, I], U32)
        part_cols = sbuf("part_cols", [P, i_tiles], F32)

        def concept_products(h):
            half = slice(h * HALF, (h + 1) * HALF)
            quantize(c_codes[:, half], c_scales[:, half], c_grouped[h][:])
            for j in range(2):
                cols = slice((2 * h + j) * P, (2 * h + j + 1) * P)
                product(b_banks[h][:, j, :], c_codes[:, cols], c_scales[:, cols], q_codes[:], q_scales[:])

        def key_products(h):
            gather_vector(picked_words[:, h * HALF : (h + 1) * HALF], key_words[:].bitcast(U32).indirect(halves_t[h]))
            for j in range(2):
                cols = slice((2 * h + j) * P, (2 * h + j + 1) * P)
                product(a_banks[h][:, j, :], picked_words[:, cols], picked_bytes[:, cols], q_codes[:], q_scales[:])

        concept_products(0)
        part_turned = bank(6, "part_turned", [P, i_tiles, P])
        for source, first_block in ((part_hi, 2), (part_lo, 0)):
            for j in range(2):
                nc.tensor.transpose(part_turned[:, first_block + j, :], source[:, j * P : (j + 1) * P], ident[:])
        load_values(3, "stage3")
        nc.scalar.copy(part_cols[:], part_turned[:, :, 0])
        key_products(0)
        concept_products(1)
        key_products(1)
        for h in range(2):
            for j in range(2):
                nc.scalar.activation(
                    scaled_b[h][:, j, :], b_banks[h][:, j, :], ACT.Copy, scale=part_cols[:, 2 * h + j : 2 * h + j + 1]
                )
            nc.vector.tensor_tensor(neg_d[h][:], scaled_b[h][:], a_banks[h][:], ALU.subtract)

        turned = bank(7, "turned", [P, P])
        nc.tensor.transpose(turned[:], rows, ident[:])
        cols_sb = sbuf("cols_sb", [P, 3 * q_tiles], F32)
        nc.vector.tensor_copy(cols_sb[:], turned[:, 0 : 3 * q_tiles])

        v_picked = []
        v_grouped = []
        v_codes = []
        v_scales = [sbuf(f"v_scales{e}", [P, P], U8) for e in range(e_tiles)]

        def gather_values(e, reuse):
            v_picked.append(sbuf(f"v_picked{e}", [P, I], BF16, reuse))
            gather_scalar(v_picked[e][:], v_raw[e][:].indirect(list_t[:]))

        def turn_values(e, reuse):
            v_grouped.append(sbuf(f"v_grouped{e}", [P, P, PACK], BF16, reuse))
            pairs = v_picked[e][:].bitcast(F32)
            pair_bank = bank(7 - e % 2, f"v_bank{e}", [P, 2, P])
            for u in range(2):
                nc.tensor.transpose(pair_bank[:, u, :], pairs[:, u : I // 2 : 2], ident[:])
            nc.scalar.copy(
                v_grouped[e][:].rearrange("s x r -> s (x r)").bitcast(F32).rearrange("s (x u) -> s x u", u=2),
                pair_bank[:].rearrange("s u x -> s x u"),
            )

        def quantize_values(e, reuse):
            v_codes.append(sbuf(f"v_codes{e}", [P, P], U32, reuse))
            quantize(v_codes[e][:], v_scales[e][:], v_grouped[e][:])

        d_banks = [bank(4 + t, f"d_bank{t}", [P, I]) for t in range(q_tiles)]
        for h in range(2):
            for t in range(q_tiles):
                for j in range(2):
                    cols = slice((2 * h + j) * P, (2 * h + j + 1) * P)
                    nc.tensor.transpose(d_banks[t][:, cols], neg_d[h][:, j, t * P : (t + 1) * P], ident[:])

        hold_bank = bank(3, "hold_bank", [P, Q])
        for t in range(q_tiles):
            nc.tensor.transpose(hold_bank[:, t * P : (t + 1) * P], cols_sb[:, 4 + t : 5 + t].to_broadcast([P, P]), ident[:])

        gather_values(0, None)
        gather_values(1, None)

        def column(name):
            return [sbuf(f"{name}{t}", [P, 1], F32) for t in range(q_tiles)]

        neg_s = [sbuf(f"neg_s{t}", [P, PACK, P], F32) for t in range(q_tiles)]
        p = []
        neg_max, p_sum, p_inv, damp, u_sum, u_inv = [
            column(n) for n in ("neg_max", "p_sum", "p_inv", "damp", "u_sum", "u_inv")
        ]
        runs = []
        damped = [sbuf(f"damped{t}", [P, I // RUN], F32) for t in range(q_tiles)]
        kk = [sbuf(f"kk{t}", [P, I // RUN, 2], F32) for t in range(q_tiles)]

        for t in range(q_tiles):
            nc.vector.tensor_scalar(
                neg_s[t][:], d_banks[t][:].rearrange("q (s r) -> q r s", r=PACK), cols_sb[:, t : t + 1], None,
                ALU.mult, ALU.min, accum_out=neg_max[t][:],
            )
        for t in range(q_tiles):
            p.append(sbuf(f"p{t}", [P, I], F32, ("stage1", "neg_s0")[t]))
            nc.scalar.activation(
                p[t][:], neg_s[t][:].rearrange("q r s -> q (r s)"), ACT.Exp, bias=neg_max[t][:], scale=-1.0,
                accum_out=p_sum[t][:],
            )
        k0 = [sbuf(f"k0{t}", [P, I // RUN], F32) for t in range(q_tiles)]
        turn_values(0, "neg_s1")
        turn_values(1, "neg_max1")
        p_banks = [bank(t, f"p_bank{t}", [P, PACK, P]) for t in range(q_tiles)]
        for t in range(q_tiles):
            for r in range(PACK):
                nc.tensor.transpose(p_banks[t][:, r, :], p[t][:, r * P : (r + 1) * P], ident[:])
        for t in range(q_tiles):
            nc.vector.reciprocal(p_inv[t][:], p_sum[t][:])
            runs.append(sbuf(f"runs{t}", [P, I // RUN], F32, ("p_sum0", "p_inv0")[t]))
            nc.vector.tensor_reduce(
                runs[t][:], p[t][:].rearrange("q (r g h) -> q g r h", r=PACK, h=2), AXIS.XY, ALU.add
            )
            nc.vector.tensor_scalar(damp[t][:], p_inv[t][:], cols_sb[:, 2 + t : 3 + t], -1.0, ALU.mult, ALU.mult)
            nc.scalar.activation(k0[t][:], runs[t][:], ACT.Exp, scale=damp[t][:])
        quantize_values(0, "p_inv1")
        scaled_p = [sbuf(f"scaled_p{t}", [P, PACK, P], F32, f"damp{t}") for t in range(q_tiles)]
        for t in range(q_tiles):
            for r in range(PACK):
                nc.scalar.activation(scaled_p[t][:, r, :], p_banks[t][:, r, :], ACT.Copy, scale=factor[:, r : r + 1])
        for t in range(q_tiles):
            nc.vector.scalar_tensor_tensor(damped[t][:], runs[t][:], 1.0, k0[t][:], ALU.mult, ALU.mult, accum_out=u_sum[t][:])
        for t in range(q_tiles):
            nc.vector.reciprocal(u_inv[t][:], u_sum[t][:])
        quantize_values(1, "u_sum0")
        k_banks = [bank(4 + t, f"k_bank{t}", [P, P]) for t in range(q_tiles)]
        for t in range(q_tiles):
            nc.vector.tensor_scalar(
                kk[t][:], k0[t][:].unsqueeze(2).to_broadcast([P, I // RUN, 2]), u_inv[t][:], None, ALU.mult
            )
        for t in range(q_tiles):
            nc.tensor.transpose(k_banks[t][:], kk[t][:].rearrange("q g h -> q (g h)"), ident[:])

        gather_values(2, "p_inv0")
        gather_values(3, "kk1")
        for e in (2, 3):
            turn_values(e, None)
            quantize_values(e, None)

        w_grouped = [sbuf(f"w_grouped{t}", [P, P, PACK], BF16) for t in range(q_tiles)]
        w_codes = sbuf("w_codes", [P, Q], U32)
        w_scales = sbuf("w_scales", [P, Q], U8)
        for t in range(q_tiles):
            nc.vector.tensor_tensor(
                w_grouped[t][:].rearrange("s (c i) r -> s c r i", i=LINE),
                scaled_p[t][:].rearrange("s r (c i) -> s c r i", i=LINE),
                k_banks[t][:].rearrange("s (c i) -> s c i", i=LINE).unsqueeze(2).to_broadcast([P, P // LINE, PACK, LINE]),
                ALU.mult,
            )
        for t in range(q_tiles):
            rows_q = slice(t * P, (t + 1) * P)
            quantize(w_codes[:, rows_q], w_scales[:, rows_q], w_grouped[t][:])

        o_bank_numbers = (2, 4, 0, 1)
        for e in range(e_tiles):
            o_bank = bank(o_bank_numbers[e], f"o_bank{e}", [P, Q])
            product(o_bank[:], v_codes[e][:], v_scales[e][:], w_codes[:], w_scales[:])
            sums = sbuf(f"sums{e}", [P, Q // GROUP], F32)
            taken = sbuf(f"taken{e}", [P, Q // GROUP, GROUP], F32)
            y = sbuf(f"y{e}", [P, Q], F32)
            nc.vector.tensor_reduce(sums[:], o_bank[:].rearrange("e (k j) -> e k j", j=GROUP), AXIS.X, ALU.add)
            nc.vector.scalar_tensor_tensor(
                taken[:], sums[:].unsqueeze(2).to_broadcast([P, Q // GROUP, GROUP]), 1.0 / GROUP,
                hold_bank[:].rearrange("e (k j) -> e k j", j=GROUP), ALU.mult, ALU.mult,
            )
            nc.vector.tensor_tensor(y[:], o_bank[:], taken[:].rearrange("e k j -> e (k j)"), ALU.subtract)
            nc.sync.dma_start(out=out[e * P : (e + 1) * P, :], in_=y[:])
